import numpy as np
import ml_dtypes


def mxq(x, axis, fmt="e4m3"):
    dtype, down = {"e4m3": (ml_dtypes.float8_e4m3fn, 7), "e5m2": (ml_dtypes.float8_e5m2, 14)}[fmt]
    v = np.moveaxis(np.asarray(x, np.float32).astype(ml_dtypes.bfloat16).astype(np.float64), axis, -1)
    blocks = v.reshape(v.shape[:-1] + (-1, 32))
    amax = np.abs(blocks).max(-1, keepdims=True)
    byte = np.maximum(np.where(amax > 0, np.frexp(amax)[1] - 1 + 127, 0) - down, 1)
    scale = np.exp2(byte - 127.0)
    codes = (blocks / scale).astype(np.float32).astype(dtype).astype(np.float64)
    return np.moveaxis((codes * scale).reshape(v.shape), -1, axis)


WIDE = False


def mx_kscale(k):
    if not WIDE:
        return np.ones(k)
    levels = np.array([10, -10, 5, -5, 0])
    if k % 512:
        return np.exp2(np.random.permutation(np.resize(levels, k // 32))).repeat(32)
    a = np.empty((k // 512, 16))
    for p in range(k // 512):
        a[p, :8] = np.random.permutation(np.resize(levels, 8))
        for g in range(8):
            far = levels[np.abs(levels - a[p, g]) >= 10]
            a[p, g + 8] = far[np.random.randint(len(far))]
    return np.exp2(a.ravel()).repeat(32)


def f64(x):
    return np.asarray(x).astype(np.float64)


def striped(idx):
    return np.tile(idx.reshape(-1, 16).T, (8, 1)).astype(np.uint16)


def unstriped(offs):
    return offs[:16].T.reshape(-1).astype(np.int64)


E2M1 = np.array([0.0, 0.5, 1.0, 1.5, 2.0, 3.0, 4.0, 6.0, -0.0, -0.5, -1.0, -1.5, -2.0, -3.0, -4.0, -6.0])


def pack_weight(w, fmt):
    k, n = w.shape
    w = f64(np.asarray(w, np.float32).astype(ml_dtypes.bfloat16)).reshape(k // 32, 32, n)
    amax = np.abs(w).max(1)
    if fmt == "e4m3":
        byte = np.frexp(amax)[1] - 1 + 127 - 7
    else:
        mant, ex = np.frexp(amax / 6.0)
        byte = np.where(mant > 0.5, ex, ex - 1) + 127
    byte = np.clip(np.where(amax > 0, byte, 1), 1, 254)
    scaled = (w * np.exp2(127.0 - byte)[:, None, :]).reshape(k, n).astype(np.float32)
    by_word = np.ascontiguousarray(scaled.reshape(k // 512, 128, 4, n).transpose(0, 1, 3, 2))
    if fmt == "e4m3":
        words = by_word.astype(ml_dtypes.float8_e4m3fn).view(np.uint8)
    else:
        c = by_word.astype(ml_dtypes.float4_e2m1fn).view(np.uint8) & 0xF
        words = (c[..., 0::2] | (c[..., 1::2] << 4)).reshape(k // 512, 128, 2 * n)
    return np.ascontiguousarray(words), np.ascontiguousarray(byte.astype(np.uint8).reshape(k // 512, 16, n))


def unpack_weight(words, scales, fmt):
    g, _, n = scales.shape
    words = np.ascontiguousarray(words).reshape(g, 128, n, -1)
    if fmt == "e4m3":
        vals = words.view(ml_dtypes.float8_e4m3fn).astype(np.float64)
    else:
        nib = np.empty((g, 128, n, 4), np.uint8)
        nib[..., 0::2] = words & 0xF
        nib[..., 1::2] = words >> 4
        vals = E2M1[nib]
    vals = vals * np.repeat(np.exp2(scales.astype(np.float64) - 127.0), 8, axis=1)[..., None]
    return vals.transpose(0, 1, 3, 2).reshape(g * 512, n)


def gelu(v):
    return 0.5 * v * (1.0 + np.tanh(np.sqrt(2.0 / np.pi) * (v + 0.044715 * v**3)))


K, T, S, S2 = 1024, 2048, 1024, 512

def setup_inputs():
    n = np.random.standard_normal
    s = mx_kscale(K)[:, None]
    d = {}
    d["tab_words"], d["tab_scales"] = pack_weight(n((K, T)) * s, "e4m3")
    d["offs"] = striped(np.random.permutation(T)[:S])
    d["offs2"] = striped(np.random.permutation(T)[:S2])
    d["w1"] = (n((K, K)) / K / s / s.T).astype(np.float32)
    d["w2_words"], d["w2_scales"] = pack_weight(n((K, K)) / K / s / s.T, "e2m1")
    d["gain"] = (1.5 * np.exp(0.4 * n(S2))).astype(np.float32)
    d["temp"] = (0.7 * n((S2, S))).astype(np.float32)
    return d

def reference(tab_words, tab_scales, offs, offs2, w1, w2_words, w2_scales, gain, temp):
    TW = unpack_weight(tab_words, tab_scales, "e4m3")
    v = TW[:, unstriped(offs)]
    v2 = TW[:, unstriped(offs2)]
    w1q = mxq(f64(w1), 0, "e4m3")
    w2 = unpack_weight(w2_words, w2_scales, "e2m1")
    a = np.abs(w1q.T @ v)
    b = np.abs(w2.T @ v)
    h = np.minimum(a, b)
    hq = mxq(h, 0, "e4m3")
    e = v2.T @ hq
    return f64(gain)[:, None] * e + f64(temp)

@@ -1,0 +1,249 @@
+from contextlib import ExitStack
+
+import concourse.mybir as mybir
+
+K, T, S, S2 = 1024, 2048, 1024, 512
+FLOPS = 2 * 2 * K * K * S + 2 * K * S2 * S
+
+F32 = mybir.dt.float32
+BF16 = mybir.dt.bfloat16
+I32 = mybir.dt.int32
+U32 = mybir.dt.uint32
+U16 = mybir.dt.uint16
+U8 = mybir.dt.uint8
+FP8X4 = mybir.dt.float8_e4m3fn_x4
+FP4X4 = mybir.dt.float4_e2m1fn_x4
+ABS = mybir.ActivationFunctionType.Abs
+COPY = mybir.ActivationFunctionType.Copy
+ALU = mybir.AluOpType
+
+P = 128
+PACK = 4
+PASS = P * PACK
+PASSES = K // PASS
+N = 512
+HALVES = S // N
+M_TILES = S2 // P
+
+
+def tile_list_grease_softening_scores_kernel(
+    tc, tab_words, tab_scales, offs, offs2, w1, w2_words, w2_scales, gain, temp, out
+):
+    nc = tc.nc
+    with ExitStack() as ctx:
+        keep = ctx.enter_context(tc.tile_pool(name="keep", bufs=1))
+        psum = ctx.enter_context(tc.psum_pool(name="psum", bufs=8))
+
+        idx = keep.tile([P, S // 16], U16, name="idx")
+        idx2 = keep.tile([P, S2 // 16], U16, name="idx2")
+        tab_plane = keep.tile([P, T], U8, name="tab_plane", tag="tab_plane", align_bytes=64)
+        w2_plane_raw = keep.tile([P, PASSES, K], U8, name="w2_plane_raw", tag="w2_plane_raw", align_bytes=64)
+        v_plane = keep.tile([P, S], U8, name="v_plane", align_bytes=64)
+        v_plane_low = keep.tile([P, S], U8, name="v_plane_low", align_bytes=64)
+        v2_plane = keep.tile([P, S2], U8, name="v2_plane", align_bytes=64)
+
+        nc.vector.memset(tab_plane[:].bitcast(I32), 0)
+        nc.gpsimd.memset(v_plane_low[:].bitcast(I32), 0)
+        with tc.tile_pool(name="zero", bufs=1) as zero_pool:
+            zero = zero_pool.tile([P, 1], I32, name="zero")
+            nc.vector.memset(zero[:], 0)
+            nc.vector.tensor_copy(
+                w2_plane_raw[:].rearrange("p a c -> p (a c)").bitcast(I32), zero[:].to_broadcast([P, PASSES * K // 4])
+            )
+        main = ctx.enter_context(tc.tile_pool(name="main", bufs=1))
+
+        def place(shape, dtype, name, tag=None):
+            pool = keep if tag in ("tab_plane", "w2_plane_raw") else main
+            return pool.tile(shape, dtype, name=name, tag=tag or name, align_bytes=64)
+
+        tab, w1_raw = {}, {}
+
+        def load_tab(a):
+            tab[a] = place([P, T], I32, "tab%d" % a)
+            nc.sync.dma_start(tab[a][:], tab_words[a].rearrange("p t i -> p (t i)").bitcast(I32))
+
+        def load_w1(a, b, tag=None):
+            w1_raw[a, b] = place([P, PACK, PASS], F32, "w1_raw%d%d" % (a, b), tag)
+            nc.sync.dma_start(
+                w1_raw[a, b][:],
+                w1[a * PASS : (a + 1) * PASS, b * PASS : (b + 1) * PASS].rearrange("(p i) c -> p i c", i=PACK),
+            )
+
+        nc.sync.dma_start(idx[:], offs)
+        nc.sync.dma_start(idx2[:], offs2)
+        for q in range(4):
+            nc.sync.dma_start(
+                tab_plane[32 * q : 32 * q + 8, :].bitcast(I32), tab_scales[:, 4 * q : 4 * q + 4, :].bitcast(I32)
+            )
+        load_tab(0)
+        load_w1(0, 0)
+        for q in range(4):
+            nc.sync.dma_start(
+                w2_plane_raw[32 * q : 32 * q + 4, :, :].bitcast(I32),
+                w2_scales[:, 4 * q : 4 * q + 4, :].rearrange("a r c -> r a c").bitcast(I32),
+            )
+        load_w1(1, 0)
+        load_tab(1)
+        w2_raw = place([P, PASSES, 2 * K], U8, "w2_raw")
+        nc.sync.dma_start(w2_raw[:].bitcast(I32), w2_words.rearrange("a p c -> p a c").bitcast(I32))
+
+        v, v2 = {}, {}
+
+        def gather_v(a, half, tag=None):
+            v[a, half] = place([P, N], U32, "v%d%d" % (a, half), tag)
+            cols = slice(half * N // 16, (half + 1) * N // 16)
+            nc.vector.tensor_copy(v[a, half][:], tab[a][:].bitcast(U32).indirect(idx[:, cols]))
+
+        def gather_v2(a, tag=None):
+            v2[a] = place([P, S2], U32, "v2_%d" % a, tag)
+            nc.vector.tensor_copy(v2[a][:], tab[a][:].bitcast(U32).indirect(idx2[:]))
+
+        def deal_w2_words(tag):
+            codes = place([P, PASSES * 2 * K], U8, "w2_codes", tag)
+            nc.vector.tensor_copy(
+                codes[:].bitcast(U16).rearrange("p (g t c i) -> p g c t i", t=PACK, c=16, i=8),
+                w2_raw[:].rearrange("p a c -> p (a c)").bitcast(U16).rearrange("p (g c i t) -> p g c t i", t=PACK, c=16, i=8),
+            )
+            return codes
+
+        def deal_w2_plane(tag):
+            plane = place([P, PASSES * K], U8, "w2_plane", tag)
+            nc.vector.tensor_copy(
+                plane[:].rearrange("p (g t c i) -> p g c t i", t=PACK, c=8, i=16),
+                w2_plane_raw[:].rearrange("p a (b c i t) -> p (a b) c t i", t=PACK, c=8, i=16),
+            )
+            return plane
+
+        w1_codes, w1_plane = {}, {}
+
+        def round_w1(a, b, dst, on_scalar):
+            dst = dst.rearrange("p (t m i) -> p m i t", t=PACK, i=PACK)
+            src = w1_raw[a, b][:].rearrange("p i (m t) -> p m i t", t=PACK)
+            if on_scalar:
+                nc.scalar.activation(dst, src, COPY)
+            else:
+                nc.vector.tensor_copy(dst, src)
+
+        def quantize_w1(b, passes, src):
+            width = len(passes) * PASS
+            codes = place([P, width], U32, "w1_codes%d%d" % (passes[0], b))
+            plane = place([P, width], U8, "w1_plane%d%d" % (passes[0], b))
+            nc.vector.quantize_mx(codes[:].bitcast(FP8X4), plane[:], src)
+            for n, a in enumerate(passes):
+                w1_codes[a, b] = codes[:, n * PASS : (n + 1) * PASS]
+                w1_plane[a, b] = plane[:, n * PASS : (n + 1) * PASS]
+
+        def response(weight, b, half):
+            resp = main.tile([P, PACK, N], F32, name="resp%d" % weight, bufs=3)
+            cols = slice(half * N, (half + 1) * N)
+            for t in range(PACK):
+                bank = psum.tile([P, N], F32, name="bank")
+                for a in range(PASSES):
+                    if weight == 1:
+                        lhs = w1_codes[a, b][:, t * P : (t + 1) * P].bitcast(FP8X4)
+                        lhs_scale = w1_plane[a, b][:, t * P : (t + 1) * P]
+                        rhs_scale = v_plane[4 * a :, cols]
+                    else:
+                        c0 = a * K + b * PASS + t * P
+                        lhs = w2_codes[:, 2 * c0 : 2 * (c0 + P)].bitcast(FP4X4)
+                        lhs_scale = w2_plane[:, c0 : c0 + P]
+                        rhs_scale = (v_plane, v_plane_low)[a][:, cols]
+                    nc.tensor.matmul_mx(
+                        bank[:], lhsT=lhs, lhsT_scale=lhs_scale,
+                        rhs=v[a, half][:].bitcast(FP8X4), rhs_scale=rhs_scale,
+                        start=(a == 0), stop=(a == PASSES - 1),
+                    )
+                nc.scalar.activation(resp[:, t, :], bank[:], ABS)
+            return resp
+
+        h_bf, h_codes, h_plane = {}, {}, {}
+
+        def smaller(b, half, r1, r2):
+            h_bf[b, half] = main.tile([P, N * PACK], BF16, name="h_bf", bufs=2, align_bytes=64)
+            nc.vector.tensor_tensor(
+                h_bf[b, half][:].rearrange("p (c i t) -> p c t i", t=PACK, i=4),
+                r1[:].rearrange("p t (c i) -> p c t i", i=4),
+                r2[:].rearrange("p t (c i) -> p c t i", i=4),
+                ALU.min,
+            )
+
+        def quantize_h(b, half):
+            h_codes[b, half] = place([P, N], U32, "h_codes%d%d" % (b, half))
+            h_plane[b, half] = place([P, N], U8, "h_plane%d%d" % (b, half))
+            nc.vector.quantize_mx(h_codes[b, half][:].bitcast(FP8X4), h_plane[b, half][:], h_bf[b, half][:])
+
+        temp_sb = {}
+
+        def load_temp(half, tag):
+            temp_sb[half] = place([P, M_TILES, N], F32, "temp%d" % half, tag)
+            nc.sync.dma_start(
+                temp_sb[half][:], temp[:, half * N : (half + 1) * N].rearrange("(c p) n -> p c n", p=P)
+            )
+
+        def load_gain(tag):
+            cols = place([P, M_TILES], F32, "gain_cols", tag)
+            with nc.allow_non_contiguous_dma(reason="one gain value to a partition"):
+                nc.sync.dma_start(cols[:], gain.rearrange("(c p) -> p c", p=P))
+            return cols
+
+        def scores(half, tiles):
+            for c in tiles:
+                bank = psum.tile([P, N], F32, name="bank")
+                for b in range(PASSES):
+                    nc.tensor.matmul_mx(
+                        bank[:], lhsT=v2[b][:, c * P : (c + 1) * P].bitcast(FP8X4),
+                        lhsT_scale=v2_plane[4 * b :, c * P : (c + 1) * P],
+                        rhs=h_codes[b, half][:].bitcast(FP8X4), rhs_scale=h_plane[b, half][:],
+                        start=(b == 0), stop=(b == PASSES - 1),
+                    )
+                res = main.tile([P, N], F32, name="res", bufs=8)
+                nc.vector.scalar_tensor_tensor(
+                    res[:], bank[:], gain_cols[:, c : c + 1], temp_sb[half][:, c, :], ALU.mult, ALU.add
+                )
+                nc.sync.dma_start(out[c * P : (c + 1) * P, half * N : (half + 1) * N], res[:])
+
+        nc.vector.tensor_copy(v_plane[:], tab_plane[:].indirect(idx[:]))
+        nc.scalar.dma_start(v_plane_low[0:112, :].bitcast(I32), v_plane[4:116, :].bitcast(I32))
+        bf00 = place([P, PACK * PASS], BF16, "bf00")
+        round_w1(0, 0, bf00[:], True)
+        gather_v(0, 0)
+        gather_v(0, 1)
+        gather_v2(0)
+        nc.vector.tensor_copy(v2_plane[:], tab_plane[:].indirect(idx2[:]))
+        load_w1(1, 1, "tab_plane")
+        load_w1(0, 1, "w1_raw00")
+        quantize_w1(0, [0], bf00[:])
+        w2_plane = deal_w2_plane("bf00")
+        bf10 = place([P, PACK * PASS], BF16, "bf10")
+        round_w1(1, 0, bf10[:], True)
+        gather_v(1, 0, "w2_plane_raw")
+        quantize_w1(0, [1], bf10[:])
+        r1_00 = response(1, 0, 0)
+        gather_v(1, 1, "w1_raw10")
+        r1_01 = response(1, 0, 1)
+        w2_codes = deal_w2_words("bf10")
+        r2_00 = response(2, 0, 0)
+        r2_01 = response(2, 0, 1)
+        bf1 = place([P, PASSES, PACK * PASS], BF16, "bf1", "w2_raw")
+        round_w1(1, 1, bf1[:, 1, :], False)
+        round_w1(0, 1, bf1[:, 0, :], False)
+        load_temp(0, "tab_plane")
+        load_temp(1, "w1_raw00")
+        quantize_w1(1, [0, 1], bf1[:].rearrange("p a c -> p (a c)"))
+        gather_v2(1, "w2_raw")
+        gain_cols = load_gain("tab1")
+        smaller(0, 0, r1_00, r2_00)
+        quantize_h(0, 0)
+        r2_10 = response(2, 1, 0)
+        r1_10 = response(1, 1, 0)
+        smaller(0, 1, r1_01, r2_01)
+        quantize_h(0, 1)
+        r2_11 = response(2, 1, 1)
+        r1_11 = response(1, 1, 1)
+        smaller(1, 0, r1_10, r2_10)
+        quantize_h(1, 0)
+        scores(0, [0, 1])
+        smaller(1, 1, r1_11, r2_11)
+        quantize_h(1, 1)
+        scores(0, [2, 3])
+        scores(1, range(M_TILES))

@@ -38,9 +38,8 @@ def tile_list_grease_softening_scores_kernel(
         idx2 = keep.tile([P, S2 // 16], U16, name="idx2")
         tab_plane = keep.tile([P, T], U8, name="tab_plane", tag="tab_plane", align_bytes=64)
         w2_plane_raw = keep.tile([P, PASSES, K], U8, name="w2_plane_raw", tag="w2_plane_raw", align_bytes=64)
-        v_plane = keep.tile([P, S], U8, name="v_plane", align_bytes=64)
         v_plane_low = keep.tile([P, S], U8, name="v_plane_low", align_bytes=64)
-        v2_plane = keep.tile([P, S2], U8, name="v2_plane", align_bytes=64)
+        w2_raw = keep.tile([P, PASSES, 2 * K], U8, name="w2_raw", tag="w2_raw", align_bytes=64)
 
         nc.vector.memset(tab_plane[:].bitcast(I32), 0)
         nc.gpsimd.memset(v_plane_low[:].bitcast(I32), 0)
@@ -53,7 +52,7 @@ def tile_list_grease_softening_scores_kernel(
         main = ctx.enter_context(tc.tile_pool(name="main", bufs=1))
 
         def place(shape, dtype, name, tag=None):
-            pool = keep if tag in ("tab_plane", "w2_plane_raw") else main
+            pool = keep if tag in ("w2_raw", "w2_plane_raw") else main
             return pool.tile(shape, dtype, name=name, tag=tag or name, align_bytes=64)
 
         tab, w1_raw = {}, {}
@@ -70,22 +69,21 @@ def tile_list_grease_softening_scores_kernel(
             )
 
         nc.sync.dma_start(idx[:], offs)
+        nc.sync.dma_start(w2_raw[:].bitcast(I32), w2_words.rearrange("a p c -> p a c").bitcast(I32))
         nc.sync.dma_start(idx2[:], offs2)
         for q in range(4):
             nc.sync.dma_start(
                 tab_plane[32 * q : 32 * q + 8, :].bitcast(I32), tab_scales[:, 4 * q : 4 * q + 4, :].bitcast(I32)
             )
-        load_tab(0)
-        load_w1(0, 0)
         for q in range(4):
             nc.sync.dma_start(
                 w2_plane_raw[32 * q : 32 * q + 4, :, :].bitcast(I32),
                 w2_scales[:, 4 * q : 4 * q + 4, :].rearrange("a r c -> r a c").bitcast(I32),
             )
-        load_w1(1, 0)
+        load_tab(0)
         load_tab(1)
-        w2_raw = place([P, PASSES, 2 * K], U8, "w2_raw")
-        nc.sync.dma_start(w2_raw[:].bitcast(I32), w2_words.rearrange("a p c -> p a c").bitcast(I32))
+        load_w1(0, 0)
+        load_w1(1, 0)
 
         v, v2 = {}, {}
 
@@ -202,36 +200,38 @@ def tile_list_grease_softening_scores_kernel(
                 )
                 nc.sync.dma_start(out[c * P : (c + 1) * P, half * N : (half + 1) * N], res[:])
 
+        w2_codes = deal_w2_words(None)
+        v_plane = place([P, S], U8, "v_plane", "w2_raw")
         nc.vector.tensor_copy(v_plane[:], tab_plane[:].indirect(idx[:]))
         nc.scalar.dma_start(v_plane_low[0:112, :].bitcast(I32), v_plane[4:116, :].bitcast(I32))
+        w2_plane = deal_w2_plane(None)
+        load_w1(1, 1, "w2_plane_raw")
+        gather_v(0, 0)
+        gather_v(1, 0)
         bf00 = place([P, PACK * PASS], BF16, "bf00")
         round_w1(0, 0, bf00[:], True)
-        gather_v(0, 0)
-        gather_v(0, 1)
-        gather_v2(0)
-        nc.vector.tensor_copy(v2_plane[:], tab_plane[:].indirect(idx2[:]))
-        load_w1(1, 1, "tab_plane")
         load_w1(0, 1, "w1_raw00")
-        quantize_w1(0, [0], bf00[:])
-        w2_plane = deal_w2_plane("bf00")
+        r2_00 = response(2, 0, 0)
+        gather_v(0, 1)
+        gather_v(1, 1)
+        r2_01 = response(2, 0, 1)
+        gather_v2(0)
         bf10 = place([P, PACK * PASS], BF16, "bf10")
-        round_w1(1, 0, bf10[:], True)
-        gather_v(1, 0, "w2_plane_raw")
+        round_w1(1, 0, bf10[:], False)
+        load_temp(0, "w1_raw10")
+        quantize_w1(0, [0], bf00[:])
         quantize_w1(0, [1], bf10[:])
         r1_00 = response(1, 0, 0)
-        gather_v(1, 1, "w1_raw10")
         r1_01 = response(1, 0, 1)
-        w2_codes = deal_w2_words("bf10")
-        r2_00 = response(2, 0, 0)
-        r2_01 = response(2, 0, 1)
-        bf1 = place([P, PASSES, PACK * PASS], BF16, "bf1", "w2_raw")
+        v2_plane = place([P, S2], U8, "v2_plane", "bf00")
+        nc.vector.tensor_copy(v2_plane[:], tab_plane[:].indirect(idx2[:]))
+        gather_v2(1, "bf10")
+        bf1 = place([P, PASSES, PACK * PASS], BF16, "bf1", "tab1")
         round_w1(1, 1, bf1[:, 1, :], False)
+        load_temp(1, "w2_plane_raw")
         round_w1(0, 1, bf1[:, 0, :], False)
-        load_temp(0, "tab_plane")
-        load_temp(1, "w1_raw00")
+        gain_cols = load_gain("w1_raw00")
         quantize_w1(1, [0, 1], bf1[:].rearrange("p a c -> p (a c)"))
-        gather_v2(1, "w2_raw")
-        gain_cols = load_gain("tab1")
         smaller(0, 0, r1_00, r2_00)
         quantize_h(0, 0)
         r2_10 = response(2, 1, 0)

@@ -14,7 +14,6 @@ U8 = mybir.dt.uint8
 FP8X4 = mybir.dt.float8_e4m3fn_x4
 FP4X4 = mybir.dt.float4_e2m1fn_x4
 ABS = mybir.ActivationFunctionType.Abs
-COPY = mybir.ActivationFunctionType.Copy
 ALU = mybir.AluOpType
 
 P = 128
@@ -39,20 +38,20 @@ def tile_list_grease_softening_scores_kernel(
         tab_plane = keep.tile([P, T], U8, name="tab_plane", tag="tab_plane", align_bytes=64)
         w2_plane_raw = keep.tile([P, PASSES, K], U8, name="w2_plane_raw", tag="w2_plane_raw", align_bytes=64)
         v_plane_low = keep.tile([P, S], U8, name="v_plane_low", align_bytes=64)
-        w2_raw = keep.tile([P, PASSES, 2 * K], U8, name="w2_raw", tag="w2_raw", align_bytes=64)
+        w2_raw = [
+            keep.tile([P, 2 * K], U8, name="w2_raw%d" % a, tag="w2_raw%d" % a, align_bytes=64) for a in range(PASSES)
+        ]
 
         nc.vector.memset(tab_plane[:].bitcast(I32), 0)
-        nc.gpsimd.memset(v_plane_low[:].bitcast(I32), 0)
         with tc.tile_pool(name="zero", bufs=1) as zero_pool:
             zero = zero_pool.tile([P, 1], I32, name="zero")
             nc.vector.memset(zero[:], 0)
-            nc.vector.tensor_copy(
-                w2_plane_raw[:].rearrange("p a c -> p (a c)").bitcast(I32), zero[:].to_broadcast([P, PASSES * K // 4])
-            )
+            nc.vector.tensor_copy(v_plane_low[:].bitcast(I32), zero[:].to_broadcast([P, S // 4]))
+        nc.vector.memset(w2_plane_raw[:].rearrange("p a c -> p (a c)").bitcast(I32), 0)
         main = ctx.enter_context(tc.tile_pool(name="main", bufs=1))
 
         def place(shape, dtype, name, tag=None):
-            pool = keep if tag in ("w2_raw", "w2_plane_raw") else main
+            pool = keep if tag in ("w2_raw0", "w2_raw1", "w2_plane_raw", "tab_plane") else main
             return pool.tile(shape, dtype, name=name, tag=tag or name, align_bytes=64)
 
         tab, w1_raw = {}, {}
@@ -61,29 +60,30 @@ def tile_list_grease_softening_scores_kernel(
             tab[a] = place([P, T], I32, "tab%d" % a)
             nc.sync.dma_start(tab[a][:], tab_words[a].rearrange("p t i -> p (t i)").bitcast(I32))
 
-        def load_w1(a, b, tag=None):
-            w1_raw[a, b] = place([P, PACK, PASS], F32, "w1_raw%d%d" % (a, b), tag)
+        def load_w1(a, b, dst):
+            w1_raw[a, b] = dst
             nc.sync.dma_start(
-                w1_raw[a, b][:],
+                dst,
                 w1[a * PASS : (a + 1) * PASS, b * PASS : (b + 1) * PASS].rearrange("(p i) c -> p i c", i=PACK),
             )
 
         nc.sync.dma_start(idx[:], offs)
-        nc.sync.dma_start(w2_raw[:].bitcast(I32), w2_words.rearrange("a p c -> p a c").bitcast(I32))
+        for a in range(PASSES):
+            nc.sync.dma_start(w2_raw[a][:].bitcast(I32), w2_words[a].bitcast(I32))
         nc.sync.dma_start(idx2[:], offs2)
         for q in range(4):
             nc.sync.dma_start(
                 tab_plane[32 * q : 32 * q + 8, :].bitcast(I32), tab_scales[:, 4 * q : 4 * q + 4, :].bitcast(I32)
             )
+        load_tab(0)
         for q in range(4):
             nc.sync.dma_start(
                 w2_plane_raw[32 * q : 32 * q + 4, :, :].bitcast(I32),
                 w2_scales[:, 4 * q : 4 * q + 4, :].rearrange("a r c -> r a c").bitcast(I32),
             )
-        load_tab(0)
         load_tab(1)
-        load_w1(0, 0)
-        load_w1(1, 0)
+        load_w1(0, 0, place([P, PACK, PASS], F32, "w1_raw00")[:])
+        load_w1(1, 0, place([P, PACK, PASS], F32, "w1_raw10")[:])
 
         v, v2 = {}, {}
 
@@ -98,10 +98,11 @@ def tile_list_grease_softening_scores_kernel(
 
         def deal_w2_words(tag):
             codes = place([P, PASSES * 2 * K], U8, "w2_codes", tag)
-            nc.vector.tensor_copy(
-                codes[:].bitcast(U16).rearrange("p (g t c i) -> p g c t i", t=PACK, c=16, i=8),
-                w2_raw[:].rearrange("p a c -> p (a c)").bitcast(U16).rearrange("p (g c i t) -> p g c t i", t=PACK, c=16, i=8),
-            )
+            for a in range(PASSES):
+                nc.vector.tensor_copy(
+                    codes[:, 2 * a * K : 2 * (a + 1) * K].bitcast(U16).rearrange("p (b t c i) -> p b c t i", t=PACK, c=16, i=8),
+                    w2_raw[a][:].bitcast(U16).rearrange("p (b c i t) -> p b c t i", t=PACK, c=16, i=8),
+                )
             return codes
 
         def deal_w2_plane(tag):
@@ -115,10 +116,10 @@ def tile_list_grease_softening_scores_kernel(
         w1_codes, w1_plane = {}, {}
 
         def round_w1(a, b, dst, on_scalar):
-            dst = dst.rearrange("p (t m i) -> p m i t", t=PACK, i=PACK)
-            src = w1_raw[a, b][:].rearrange("p i (m t) -> p m i t", t=PACK)
+            dst = dst.rearrange("p (t m u e) -> p m u t e", t=PACK, u=2, e=2)
+            src = w1_raw[a, b].rearrange("p (u e) (m t) -> p m u t e", t=PACK, e=2)
             if on_scalar:
-                nc.scalar.activation(dst, src, COPY)
+                nc.scalar.copy(dst, src)
             else:
                 nc.vector.tensor_copy(dst, src)
 
@@ -157,16 +158,16 @@ def tile_list_grease_softening_scores_kernel(
         h_bf, h_codes, h_plane = {}, {}, {}
 
         def smaller(b, half, r1, r2):
-            h_bf[b, half] = main.tile([P, N * PACK], BF16, name="h_bf", bufs=2, align_bytes=64)
+            h_bf[b, half] = place([P, N * PACK], BF16, "h_bf%d%d" % (b, half))
             nc.vector.tensor_tensor(
-                h_bf[b, half][:].rearrange("p (c i t) -> p c t i", t=PACK, i=4),
-                r1[:].rearrange("p t (c i) -> p c t i", i=4),
-                r2[:].rearrange("p t (c i) -> p c t i", i=4),
+                h_bf[b, half][:].rearrange("p (c i t) -> p c t i", t=PACK, i=2),
+                r1[:].rearrange("p t (c i) -> p c t i", i=2),
+                r2[:].rearrange("p t (c i) -> p c t i", i=2),
                 ALU.min,
             )
 
-        def quantize_h(b, half):
-            h_codes[b, half] = place([P, N], U32, "h_codes%d%d" % (b, half))
+        def quantize_h(b, half, tag=None):
+            h_codes[b, half] = place([P, N], U32, "h_codes%d%d" % (b, half), tag)
             h_plane[b, half] = place([P, N], U8, "h_plane%d%d" % (b, half))
             nc.vector.quantize_mx(h_codes[b, half][:].bitcast(FP8X4), h_plane[b, half][:], h_bf[b, half][:])
 
@@ -201,47 +202,48 @@ def tile_list_grease_softening_scores_kernel(
                 nc.sync.dma_start(out[c * P : (c + 1) * P, half * N : (half + 1) * N], res[:])
 
         w2_codes = deal_w2_words(None)
-        v_plane = place([P, S], U8, "v_plane", "w2_raw")
+        v2_plane = place([P, S2], U8, "v2_plane", "w2_raw0")
+        nc.vector.tensor_copy(v2_plane[:], tab_plane[:].indirect(idx2[:]))
+        v_plane = place([P, S], U8, "v_plane", "w2_raw1")
         nc.vector.tensor_copy(v_plane[:], tab_plane[:].indirect(idx[:]))
         nc.scalar.dma_start(v_plane_low[0:112, :].bitcast(I32), v_plane[4:116, :].bitcast(I32))
-        w2_plane = deal_w2_plane(None)
-        load_w1(1, 1, "w2_plane_raw")
+        w2_plane = deal_w2_plane("tab_plane")
+        w1_raw_late = place([P, PASSES, PACK, PASS], F32, "w1_raw_late", "w2_plane_raw")
+        load_w1(1, 1, w1_raw_late[:, 1])
+        load_w1(0, 1, w1_raw_late[:, 0])
         gather_v(0, 0)
         gather_v(1, 0)
         bf00 = place([P, PACK * PASS], BF16, "bf00")
         round_w1(0, 0, bf00[:], True)
-        load_w1(0, 1, "w1_raw00")
+        load_temp(0, "w1_raw00")
         r2_00 = response(2, 0, 0)
         gather_v(0, 1)
         gather_v(1, 1)
         r2_01 = response(2, 0, 1)
-        gather_v2(0)
         bf10 = place([P, PACK * PASS], BF16, "bf10")
         round_w1(1, 0, bf10[:], False)
-        load_temp(0, "w1_raw10")
+        load_temp(1, "w1_raw10")
         quantize_w1(0, [0], bf00[:])
         quantize_w1(0, [1], bf10[:])
         r1_00 = response(1, 0, 0)
         r1_01 = response(1, 0, 1)
-        v2_plane = place([P, S2], U8, "v2_plane", "bf00")
-        nc.vector.tensor_copy(v2_plane[:], tab_plane[:].indirect(idx2[:]))
+        gather_v2(0, "bf00")
         gather_v2(1, "bf10")
         bf1 = place([P, PASSES, PACK * PASS], BF16, "bf1", "tab1")
         round_w1(1, 1, bf1[:, 1, :], False)
-        load_temp(1, "w2_plane_raw")
         round_w1(0, 1, bf1[:, 0, :], False)
-        gain_cols = load_gain("w1_raw00")
+        gain_cols = load_gain("w2_plane_raw")
         quantize_w1(1, [0, 1], bf1[:].rearrange("p a c -> p (a c)"))
         smaller(0, 0, r1_00, r2_00)
-        quantize_h(0, 0)
         r2_10 = response(2, 1, 0)
         r1_10 = response(1, 1, 0)
         smaller(0, 1, r1_01, r2_01)
-        quantize_h(0, 1)
+        quantize_h(0, 0)
         r2_11 = response(2, 1, 1)
         r1_11 = response(1, 1, 1)
         smaller(1, 0, r1_10, r2_10)
         quantize_h(1, 0)
+        quantize_h(0, 1, "h_bf10")
         scores(0, [0, 1])
         smaller(1, 1, r1_11, r2_11)
         quantize_h(1, 1)

@@ -14,6 +14,7 @@ U8 = mybir.dt.uint8
 FP8X4 = mybir.dt.float8_e4m3fn_x4
 FP4X4 = mybir.dt.float4_e2m1fn_x4
 ABS = mybir.ActivationFunctionType.Abs
+COPY = mybir.ActivationFunctionType.Copy
 ALU = mybir.AluOpType
 
 P = 128
@@ -83,7 +84,6 @@ def tile_list_grease_softening_scores_kernel(
             )
         load_tab(1)
         load_w1(0, 0, place([P, PACK, PASS], F32, "w1_raw00")[:])
-        load_w1(1, 0, place([P, PACK, PASS], F32, "w1_raw10")[:])
 
         v, v2 = {}, {}
 
@@ -96,14 +96,13 @@ def tile_list_grease_softening_scores_kernel(
             v2[a] = place([P, S2], U32, "v2_%d" % a, tag)
             nc.vector.tensor_copy(v2[a][:], tab[a][:].bitcast(U32).indirect(idx2[:]))
 
-        def deal_w2_words(tag):
-            codes = place([P, PASSES * 2 * K], U8, "w2_codes", tag)
-            for a in range(PASSES):
-                nc.vector.tensor_copy(
-                    codes[:, 2 * a * K : 2 * (a + 1) * K].bitcast(U16).rearrange("p (b t c i) -> p b c t i", t=PACK, c=16, i=8),
-                    w2_raw[a][:].bitcast(U16).rearrange("p (b c i t) -> p b c t i", t=PACK, c=16, i=8),
-                )
-            return codes
+        w2_codes = place([P, PASSES * 2 * K], U8, "w2_codes")
+
+        def deal_w2_words(a):
+            nc.vector.tensor_copy(
+                w2_codes[:, 2 * a * K : 2 * (a + 1) * K].bitcast(U16).rearrange("p (b t c i) -> p b c t i", t=PACK, c=16, i=8),
+                w2_raw[a][:].bitcast(U16).rearrange("p (b c i t) -> p b c t i", t=PACK, c=16, i=8),
+            )
 
         def deal_w2_plane(tag):
             plane = place([P, PASSES * K], U8, "w2_plane", tag)
@@ -116,10 +115,10 @@ def tile_list_grease_softening_scores_kernel(
         w1_codes, w1_plane = {}, {}
 
         def round_w1(a, b, dst, on_scalar):
-            dst = dst.rearrange("p (t m u e) -> p m u t e", t=PACK, u=2, e=2)
-            src = w1_raw[a, b].rearrange("p (u e) (m t) -> p m u t e", t=PACK, e=2)
+            dst = dst.rearrange("p (t m i) -> p m i t", t=PACK, i=PACK)
+            src = w1_raw[a, b].rearrange("p i (m t) -> p m i t", t=PACK)
             if on_scalar:
-                nc.scalar.copy(dst, src)
+                nc.scalar.activation(dst, src, COPY)
             else:
                 nc.vector.tensor_copy(dst, src)
 
@@ -160,9 +159,9 @@ def tile_list_grease_softening_scores_kernel(
         def smaller(b, half, r1, r2):
             h_bf[b, half] = place([P, N * PACK], BF16, "h_bf%d%d" % (b, half))
             nc.vector.tensor_tensor(
-                h_bf[b, half][:].rearrange("p (c i t) -> p c t i", t=PACK, i=2),
-                r1[:].rearrange("p t (c i) -> p c t i", i=2),
-                r2[:].rearrange("p t (c i) -> p c t i", i=2),
+                h_bf[b, half][:].rearrange("p (c i t) -> p c t i", t=PACK, i=4),
+                r1[:].rearrange("p t (c i) -> p c t i", i=4),
+                r2[:].rearrange("p t (c i) -> p c t i", i=4),
                 ALU.min,
             )
 
@@ -201,13 +200,15 @@ def tile_list_grease_softening_scores_kernel(
                 )
                 nc.sync.dma_start(out[c * P : (c + 1) * P, half * N : (half + 1) * N], res[:])
 
-        w2_codes = deal_w2_words(None)
-        v2_plane = place([P, S2], U8, "v2_plane", "w2_raw0")
-        nc.vector.tensor_copy(v2_plane[:], tab_plane[:].indirect(idx2[:]))
-        v_plane = place([P, S], U8, "v_plane", "w2_raw1")
+        deal_w2_words(0)
+        v_plane = place([P, S], U8, "v_plane")
         nc.vector.tensor_copy(v_plane[:], tab_plane[:].indirect(idx[:]))
-        nc.scalar.dma_start(v_plane_low[0:112, :].bitcast(I32), v_plane[4:116, :].bitcast(I32))
-        w2_plane = deal_w2_plane("tab_plane")
+        nc.sync.dma_start(v_plane_low[0:112, :].bitcast(I32), v_plane[4:116, :].bitcast(I32))
+        deal_w2_words(1)
+        load_w1(1, 0, place([P, PACK, PASS], F32, "w1_raw10", "w2_raw1")[:])
+        v2_plane = place([P, S2], U8, "v2_plane")
+        nc.vector.tensor_copy(v2_plane[:], tab_plane[:].indirect(idx2[:]))
+        w2_plane = deal_w2_plane(None)
         w1_raw_late = place([P, PASSES, PACK, PASS], F32, "w1_raw_late", "w2_plane_raw")
         load_w1(1, 1, w1_raw_late[:, 1])
         load_w1(0, 1, w1_raw_late[:, 0])
@@ -222,7 +223,7 @@ def tile_list_grease_softening_scores_kernel(
         r2_01 = response(2, 0, 1)
         bf10 = place([P, PACK * PASS], BF16, "bf10")
         round_w1(1, 0, bf10[:], False)
-        load_temp(1, "w1_raw10")
+        load_temp(1, "w2_raw1")
         quantize_w1(0, [0], bf00[:])
         quantize_w1(0, [1], bf10[:])
         r1_00 = response(1, 0, 0)

from contextlib import ExitStack

import concourse.mybir as mybir

K, T, S, S2 = 1024, 2048, 1024, 512
FLOPS = 2 * 2 * K * K * S + 2 * K * S2 * S

F32 = mybir.dt.float32
BF16 = mybir.dt.bfloat16
I32 = mybir.dt.int32
U32 = mybir.dt.uint32
U16 = mybir.dt.uint16
U8 = mybir.dt.uint8
FP8X4 = mybir.dt.float8_e4m3fn_x4
FP4X4 = mybir.dt.float4_e2m1fn_x4
ABS = mybir.ActivationFunctionType.Abs
COPY = mybir.ActivationFunctionType.Copy
ALU = mybir.AluOpType

P = 128
PACK = 4
PASS = P * PACK
PASSES = K // PASS
N = 512
HALVES = S // N
M_TILES = S2 // P


def tile_list_grease_softening_scores_kernel(
    tc, tab_words, tab_scales, offs, offs2, w1, w2_words, w2_scales, gain, temp, out
):
    nc = tc.nc
    with ExitStack() as ctx:
        keep = ctx.enter_context(tc.tile_pool(name="keep", bufs=1))
        psum = ctx.enter_context(tc.psum_pool(name="psum", bufs=8))

        idx = keep.tile([P, S // 16], U16, name="idx")
        idx2 = keep.tile([P, S2 // 16], U16, name="idx2")
        tab_plane = keep.tile([P, T], U8, name="tab_plane", tag="tab_plane", align_bytes=64)
        w2_plane_raw = keep.tile([P, PASSES, K], U8, name="w2_plane_raw", tag="w2_plane_raw", align_bytes=64)
        v_plane_low = keep.tile([P, S], U8, name="v_plane_low", align_bytes=64)
        w2_raw = [
            keep.tile([P, 2 * K], U8, name="w2_raw%d" % a, tag="w2_raw%d" % a, align_bytes=64) for a in range(PASSES)
        ]

        nc.vector.memset(tab_plane[:].bitcast(I32), 0)
        with tc.tile_pool(name="zero", bufs=1) as zero_pool:
            zero = zero_pool.tile([P, 1], I32, name="zero")
            nc.vector.memset(zero[:], 0)
            nc.vector.tensor_copy(v_plane_low[:].bitcast(I32), zero[:].to_broadcast([P, S // 4]))
        nc.vector.memset(w2_plane_raw[:].rearrange("p a c -> p (a c)").bitcast(I32), 0)
        main = ctx.enter_context(tc.tile_pool(name="main", bufs=1))

        def place(shape, dtype, name, tag=None):
            pool = keep if tag in ("w2_raw0", "w2_raw1", "w2_plane_raw", "tab_plane") else main
            return pool.tile(shape, dtype, name=name, tag=tag or name, align_bytes=64)

        tab, w1_raw = {}, {}

        def load_tab(a):
            tab[a] = place([P, T], I32, "tab%d" % a)
            nc.sync.dma_start(tab[a][:], tab_words[a].rearrange("p t i -> p (t i)").bitcast(I32))

        def load_w1(a, b, dst):
            w1_raw[a, b] = dst
            nc.sync.dma_start(
                dst,
                w1[a * PASS : (a + 1) * PASS, b * PASS : (b + 1) * PASS].rearrange("(p i) c -> p i c", i=PACK),
            )

        nc.sync.dma_start(idx[:], offs)
        for a in range(PASSES):
            nc.sync.dma_start(w2_raw[a][:].bitcast(I32), w2_words[a].bitcast(I32))
        nc.sync.dma_start(idx2[:], offs2)
        for q in range(4):
            nc.sync.dma_start(
                tab_plane[32 * q : 32 * q + 8, :].bitcast(I32), tab_scales[:, 4 * q : 4 * q + 4, :].bitcast(I32)
            )
        load_tab(0)
        for q in range(4):
            nc.sync.dma_start(
                w2_plane_raw[32 * q : 32 * q + 4, :, :].bitcast(I32),
                w2_scales[:, 4 * q : 4 * q + 4, :].rearrange("a r c -> r a c").bitcast(I32),
            )
        load_tab(1)
        load_w1(0, 0, place([P, PACK, PASS], F32, "w1_raw00")[:])

        v, v2 = {}, {}

        def gather_v(a, half, tag=None):
            v[a, half] = place([P, N], U32, "v%d%d" % (a, half), tag)
            cols = slice(half * N // 16, (half + 1) * N // 16)
            nc.vector.tensor_copy(v[a, half][:], tab[a][:].bitcast(U32).indirect(idx[:, cols]))

        def gather_v2(a, tag=None):
            v2[a] = place([P, S2], U32, "v2_%d" % a, tag)
            nc.vector.tensor_copy(v2[a][:], tab[a][:].bitcast(U32).indirect(idx2[:]))

        w2_codes = place([P, PASSES * 2 * K], U8, "w2_codes")

        def deal_w2_words(a):
            nc.vector.tensor_copy(
                w2_codes[:, 2 * a * K : 2 * (a + 1) * K].bitcast(U16).rearrange("p (b t c i) -> p b c t i", t=PACK, c=16, i=8),
                w2_raw[a][:].bitcast(U16).rearrange("p (b c i t) -> p b c t i", t=PACK, c=16, i=8),
            )

        def deal_w2_plane(tag):
            plane = place([P, PASSES * K], U8, "w2_plane", tag)
            nc.vector.tensor_copy(
                plane[:].rearrange("p (g t c i) -> p g c t i", t=PACK, c=8, i=16),
                w2_plane_raw[:].rearrange("p a (b c i t) -> p (a b) c t i", t=PACK, c=8, i=16),
            )
            return plane

        w1_codes, w1_plane = {}, {}

        def round_w1(a, b, dst, on_scalar):
            dst = dst.rearrange("p (t m i) -> p m i t", t=PACK, i=PACK)
            src = w1_raw[a, b].rearrange("p i (m t) -> p m i t", t=PACK)
            if on_scalar:
                nc.scalar.activation(dst, src, COPY)
            else:
                nc.vector.tensor_copy(dst, src)

        def quantize_w1(b, passes, src):
            width = len(passes) * PASS
            codes = place([P, width], U32, "w1_codes%d%d" % (passes[0], b))
            plane = place([P, width], U8, "w1_plane%d%d" % (passes[0], b))
            nc.vector.quantize_mx(codes[:].bitcast(FP8X4), plane[:], src)
            for n, a in enumerate(passes):
                w1_codes[a, b] = codes[:, n * PASS : (n + 1) * PASS]
                w1_plane[a, b] = plane[:, n * PASS : (n + 1) * PASS]

        def response(weight, b, half):
            resp = main.tile([P, PACK, N], F32, name="resp%d" % weight, bufs=3)
            cols = slice(half * N, (half + 1) * N)
            for t in range(PACK):
                bank = psum.tile([P, N], F32, name="bank")
                for a in range(PASSES):
                    if weight == 1:
                        lhs = w1_codes[a, b][:, t * P : (t + 1) * P].bitcast(FP8X4)
                        lhs_scale = w1_plane[a, b][:, t * P : (t + 1) * P]
                        rhs_scale = v_plane[4 * a :, cols]
                    else:
                        c0 = a * K + b * PASS + t * P
                        lhs = w2_codes[:, 2 * c0 : 2 * (c0 + P)].bitcast(FP4X4)
                        lhs_scale = w2_plane[:, c0 : c0 + P]
                        rhs_scale = (v_plane, v_plane_low)[a][:, cols]
                    nc.tensor.matmul_mx(
                        bank[:], lhsT=lhs, lhsT_scale=lhs_scale,
                        rhs=v[a, half][:].bitcast(FP8X4), rhs_scale=rhs_scale,
                        start=(a == 0), stop=(a == PASSES - 1),
                    )
                nc.scalar.activation(resp[:, t, :], bank[:], ABS)
            return resp

        h_bf, h_codes, h_plane = {}, {}, {}

        def smaller(b, half, r1, r2):
            h_bf[b, half] = place([P, N * PACK], BF16, "h_bf%d%d" % (b, half))
            nc.vector.tensor_tensor(
                h_bf[b, half][:].rearrange("p (c i t) -> p c t i", t=PACK, i=4),
                r1[:].rearrange("p t (c i) -> p c t i", i=4),
                r2[:].rearrange("p t (c i) -> p c t i", i=4),
                ALU.min,
            )

        def quantize_h(b, half, tag=None):
            h_codes[b, half] = place([P, N], U32, "h_codes%d%d" % (b, half), tag)
            h_plane[b, half] = place([P, N], U8, "h_plane%d%d" % (b, half))
            nc.vector.quantize_mx(h_codes[b, half][:].bitcast(FP8X4), h_plane[b, half][:], h_bf[b, half][:])

        temp_sb = {}

        def load_temp(half, tag):
            temp_sb[half] = place([P, M_TILES, N], F32, "temp%d" % half, tag)
            nc.sync.dma_start(
                temp_sb[half][:], temp[:, half * N : (half + 1) * N].rearrange("(c p) n -> p c n", p=P)
            )

        def load_gain(tag):
            cols = place([P, M_TILES], F32, "gain_cols", tag)
            with nc.allow_non_contiguous_dma(reason="one gain value to a partition"):
                nc.sync.dma_start(cols[:], gain.rearrange("(c p) -> p c", p=P))
            return cols

        def scores(half, tiles):
            for c in tiles:
                bank = psum.tile([P, N], F32, name="bank")
                for b in range(PASSES):
                    nc.tensor.matmul_mx(
                        bank[:], lhsT=v2[b][:, c * P : (c + 1) * P].bitcast(FP8X4),
                        lhsT_scale=v2_plane[4 * b :, c * P : (c + 1) * P],
                        rhs=h_codes[b, half][:].bitcast(FP8X4), rhs_scale=h_plane[b, half][:],
                        start=(b == 0), stop=(b == PASSES - 1),
                    )
                res = main.tile([P, N], F32, name="res", bufs=8)
                nc.vector.scalar_tensor_tensor(
                    res[:], bank[:], gain_cols[:, c : c + 1], temp_sb[half][:, c, :], ALU.mult, ALU.add
                )
                nc.sync.dma_start(out[c * P : (c + 1) * P, half * N : (half + 1) * N], res[:])

        deal_w2_words(0)
        v_plane = place([P, S], U8, "v_plane")
        nc.vector.tensor_copy(v_plane[:], tab_plane[:].indirect(idx[:]))
        nc.sync.dma_start(v_plane_low[0:112, :].bitcast(I32), v_plane[4:116, :].bitcast(I32))
        deal_w2_words(1)
        load_w1(1, 0, place([P, PACK, PASS], F32, "w1_raw10", "w2_raw1")[:])
        v2_plane = place([P, S2], U8, "v2_plane")
        nc.vector.tensor_copy(v2_plane[:], tab_plane[:].indirect(idx2[:]))
        w2_plane = deal_w2_plane(None)
        w1_raw_late = place([P, PASSES, PACK, PASS], F32, "w1_raw_late", "w2_plane_raw")
        load_w1(1, 1, w1_raw_late[:, 1])
        load_w1(0, 1, w1_raw_late[:, 0])
        gather_v(0, 0)
        gather_v(1, 0)
        bf00 = place([P, PACK * PASS], BF16, "bf00")
        round_w1(0, 0, bf00[:], True)
        load_temp(0, "w1_raw00")
        r2_00 = response(2, 0, 0)
        gather_v(0, 1)
        gather_v(1, 1)
        r2_01 = response(2, 0, 1)
        bf10 = place([P, PACK * PASS], BF16, "bf10")
        round_w1(1, 0, bf10[:], False)
        load_temp(1, "w2_raw1")
        quantize_w1(0, [0], bf00[:])
        quantize_w1(0, [1], bf10[:])
        r1_00 = response(1, 0, 0)
        r1_01 = response(1, 0, 1)
        gather_v2(0, "bf00")
        gather_v2(1, "bf10")
        bf1 = place([P, PASSES, PACK * PASS], BF16, "bf1", "tab1")
        round_w1(1, 1, bf1[:, 1, :], False)
        round_w1(0, 1, bf1[:, 0, :], False)
        gain_cols = load_gain("w2_plane_raw")
        quantize_w1(1, [0, 1], bf1[:].rearrange("p a c -> p (a c)"))
        smaller(0, 0, r1_00, r2_00)
        r2_10 = response(2, 1, 0)
        r1_10 = response(1, 1, 0)
        smaller(0, 1, r1_01, r2_01)
        quantize_h(0, 0)
        r2_11 = response(2, 1, 1)
        r1_11 = response(1, 1, 1)
        smaller(1, 0, r1_10, r2_10)
        quantize_h(1, 0)
        quantize_h(0, 1, "h_bf10")
        scores(0, [0, 1])
        smaller(1, 1, r1_11, r2_11)
        quantize_h(1, 1)
        scores(0, [2, 3])
        scores(1, range(M_TILES))
